import numpy as np
import ml_dtypes


def mxq(x, axis, fmt="e4m3"):
    dtype, down = {"e4m3": (ml_dtypes.float8_e4m3fn, 7), "e5m2": (ml_dtypes.float8_e5m2, 14)}[fmt]
    v = np.moveaxis(np.asarray(x, np.float32).astype(ml_dtypes.bfloat16).astype(np.float64), axis, -1)
    blocks = v.reshape(v.shape[:-1] + (-1, 32))
    amax = np.abs(blocks).max(-1, keepdims=True)
    byte = np.maximum(np.where(amax > 0, np.frexp(amax)[1] - 1 + 127, 0) - down, 1)
    scale = np.exp2(byte - 127.0)
    codes = (blocks / scale).astype(np.float32).astype(dtype).astype(np.float64)
    return np.moveaxis((codes * scale).reshape(v.shape), -1, axis)


WIDE = False


def mx_kscale(k):
    if not WIDE:
        return np.ones(k)
    levels = np.array([10, -10, 5, -5, 0])
    if k % 512:
        return np.exp2(np.random.permutation(np.resize(levels, k // 32))).repeat(32)
    a = np.empty((k // 512, 16))
    for p in range(k // 512):
        a[p, :8] = np.random.permutation(np.resize(levels, 8))
        for g in range(8):
            far = levels[np.abs(levels - a[p, g]) >= 10]
            a[p, g + 8] = far[np.random.randint(len(far))]
    return np.exp2(a.ravel()).repeat(32)


BF16 = ml_dtypes.bfloat16


def bf(x):
    return np.asarray(x, np.float32).astype(BF16)


def f64(x):
    return np.asarray(x).astype(np.float64)


E2M1 = np.array([0.0, 0.5, 1.0, 1.5, 2.0, 3.0, 4.0, 6.0, -0.0, -0.5, -1.0, -1.5, -2.0, -3.0, -4.0, -6.0])


def pack_weight(w, fmt):
    k, n = w.shape
    w = f64(bf(w)).reshape(k // 32, 32, n)
    amax = np.abs(w).max(1)
    if fmt == "e4m3":
        byte = np.frexp(amax)[1] - 1 + 127 - 7
    else:
        mant, ex = np.frexp(amax / 6.0)
        byte = np.where(mant > 0.5, ex, ex - 1) + 127
    byte = np.clip(np.where(amax > 0, byte, 1), 1, 254)
    scaled = (w * np.exp2(127.0 - byte)[:, None, :]).reshape(k, n).astype(np.float32)
    by_word = np.ascontiguousarray(scaled.reshape(k // 512, 128, 4, n).transpose(0, 1, 3, 2))
    if fmt == "e4m3":
        words = by_word.astype(ml_dtypes.float8_e4m3fn).view(np.uint8)
    else:
        c = by_word.astype(ml_dtypes.float4_e2m1fn).view(np.uint8) & 0xF
        words = c[..., 0::2] | (c[..., 1::2] << 4)
    return np.ascontiguousarray(words), np.ascontiguousarray(byte.astype(np.uint8).reshape(k // 512, 16, n))


def unpack_weight(words, scales, fmt):
    g, p, n, _ = words.shape
    if fmt == "e4m3":
        vals = np.ascontiguousarray(words).view(ml_dtypes.float8_e4m3fn).astype(np.float64)
    else:
        nib = np.empty((g, p, n, 4), np.uint8)
        nib[..., 0::2] = words & 0xF
        nib[..., 1::2] = words >> 4
        vals = E2M1[nib]
    vals = vals * np.repeat(np.exp2(scales.astype(np.float64) - 127.0), 8, axis=1)[..., None]
    return vals.transpose(0, 1, 3, 2).reshape(g * 512, n)
def pack4(w):
    words, scales = pack_weight(w, "e2m1")
    return words.reshape(words.shape[0], 128, -1), scales


def unpack4(words, scales):
    return unpack_weight(words.reshape(words.shape[0], 128, -1, 2), scales, "e2m1")


def planes(Y):
    n, m = Y.shape
    b = f64(bf(Y)).reshape(n // 32, 32, m)
    amax = np.abs(b).max(1)
    byte = np.clip(np.where(amax > 0, np.frexp(amax)[1] - 1 + 127 - 7, 1), 1, 254)
    codes = (b * np.exp2(127.0 - byte)[:, None, :]).reshape(n, m).astype(np.float32).astype(ml_dtypes.float8_e4m3fn).view(np.uint8)
    words = codes.reshape(n // 512, 128, 4, m).transpose(0, 1, 3, 2)
    return np.ascontiguousarray(words), np.ascontiguousarray(byte.astype(np.uint8).reshape(n // 512, 16, m))


N, V, D, M = 1024, 2048, 512, 512

K1, B = 1.2, 0.75
THRESHOLD = 0.3


def setup_inputs():
    s, t = mx_kscale(D), mx_kscale(V)
    tf = bf(np.random.uniform(0.0, 2.0, (N, V)))
    z = bf(np.random.standard_normal((N, D)) * s[None, :])
    e = np.random.standard_normal((V, D)) / np.sqrt(D) / s[None, :]
    e_words, e_scales = pack4(e.T)
    return {"tf": tf,
            "z": z,
            "e_words": e_words,
            "e_scales": e_scales,
            "r": bf(np.random.uniform(0.3, 2.0, N)),
            "idf": bf(np.random.standard_normal(V) * t),
            "q": bf(np.random.standard_normal((M, V)) / np.sqrt(V) / t[None, :])}


def extended_term_frequency(tf, z, e):
    sim = mxq(z, 1, "e4m3") @ e.T
    return tf + np.maximum(sim - THRESHOLD, 0.0)


def bm25_saturation(t, r):
    n = K1 * (1.0 - B + B * r)
    return 2.2 * t / (t + n[:, None])


def core(tf, z, e_words, e_scales, r, idf, q):
    t = extended_term_frequency(f64(tf), f64(z), unpack4(e_words, e_scales).T)
    b = bm25_saturation(t, f64(r))
    g = f64(idf)[None, :] * b
    return mxq(f64(q), 1, "e4m3") @ mxq(g, 1, "e4m3").T


def reference(tf, z, e_words, e_scales, r, idf, q):
    R_out = core(tf, z, e_words, e_scales, r, idf, q)
    words, scales = planes(R_out.T)
    return R_out, words, scales

@@ -1,0 +1,351 @@
+from contextlib import ExitStack
+
+import concourse.mybir as mybir
+from concourse.masks import make_identity
+
+N, V, D, M = 1024, 2048, 512, 512
+FLOPS = 2 * N * D * V + 2 * M * V * N
+
+F32 = mybir.dt.float32
+BF16 = mybir.dt.bfloat16
+U32 = mybir.dt.uint32
+I32 = mybir.dt.int32
+U8 = mybir.dt.uint8
+FP8X4 = mybir.dt.float8_e4m3fn_x4
+FP4X4 = mybir.dt.float4_e2m1fn_x4
+ALU = mybir.AluOpType
+ACT = mybir.ActivationFunctionType
+
+P = 128
+G_DOCS = 512
+NG = N // G_DOCS
+NC = V // 512
+BLOCKS = NG * NC * 4
+
+
+def tile_embeddingthresholdexpandedbm25scores_x2_kernel(tc, tf, z, e_words, e_scales, r, idf, q, out_0, out_1, out_2):
+    nc = tc.nc
+    with ExitStack() as ctx:
+        keep = ctx.enter_context(tc.tile_pool(name="keep", bufs=1))
+        work = ctx.enter_context(tc.tile_pool(name="work", bufs=3))
+        ps_s = ctx.enter_context(tc.psum_pool(name="ps_s", bufs=2))
+        ps_x = ctx.enter_context(tc.psum_pool(name="ps_x", bufs=2))
+        ps_a = ctx.enter_context(tc.psum_pool(name="ps_a", bufs=4))
+        ctx.enter_context(tc.manual_schedule())
+
+        z_sb = []
+        tf_sb = []
+        q_sb = []
+        zg, zc, zs = [], [], []
+        for g in range(NG):
+            z_sb.append(keep.tile([P, 4, D], BF16, name="z_sb%d" % g, align_bytes=64))
+            tf_sb.append([keep.tile([P, 4, 512], BF16, name="tf%d_%d" % (g, c), align_bytes=64) for c in range(NC)])
+            zg.append(keep.tile([P, 512, 4], BF16, name="zg%d" % g, align_bytes=64))
+            zc.append(keep.tile([P, 512], U32, name="zc%d" % g, align_bytes=64))
+            zs.append(keep.tile([P, 512], U8, name="zs%d" % g, align_bytes=64))
+        for h in range(2):
+            q_sb.append(keep.tile([P, 2, V], BF16, name="q_sb%d" % h, align_bytes=64))
+        e_sb = keep.tile([P, 2 * V], U8, name="e_sb", align_bytes=64)
+        es_sb = keep.tile([P, V], U8, name="es_sb", align_bytes=64)
+        ident = keep.tile([P, P], F32, name="ident")
+        r_sb = keep.tile([P, NG, 4], BF16, name="r_sb")
+        idf_sb = keep.tile([P, NC, 4], BF16, name="idf_sb")
+        dummy = keep.tile([P, 1], F32, name="dummy")
+        nlen = keep.tile([P, NG * 4], F32, name="nlen")
+        nlen2 = keep.tile([P, NG * 4], F32, name="nlen2")
+        invn = keep.tile([P, NG * 4], F32, name="invn")
+        sinv = keep.tile([P, NG * 4], F32, name="sinv")
+        binv = keep.tile([P, NG * 4], F32, name="binv")
+        idfn = keep.tile([P, NC, 4], F32, name="idfn")
+
+        tf_v = tf.rearrange("(g p t) v -> g p t v", p=P, t=4)
+        z_v = z.rearrange("(g p t) k -> g p t k", p=P, t=4)
+        q_v = q.rearrange("(h t p) v -> h p t v", p=P, t=2)
+        nc.vector.memset(dummy[:], 1.0)
+        nc.vector.memset(es_sb[:].bitcast(I32), 0)
+        nc.scalar.dma_start(out=r_sb[:], in_=r.rearrange("(g p t) -> p g t", p=P, t=4))
+        for qd in range(4):
+            nc.scalar.dma_start(
+                out=es_sb[32 * qd : 32 * qd + 4, :].bitcast(I32),
+                in_=e_scales[0][4 * qd : 4 * qd + 4, :].bitcast(I32),
+            )
+        nc.scalar.dma_start(out=idf_sb[:], in_=idf.rearrange("(c p t) -> p c t", p=P, t=4))
+        make_identity(nc, ident[:])
+        nc.sync.dma_start(out=z_sb[0][:, 0, :], in_=z_v[0][:, 0, :])
+        nc.sync.dma_start(out=e_sb[:, 0:1024].bitcast(I32), in_=e_words[0][:, 0:1024].bitcast(I32))
+        nc.sync.dma_start(out=z_sb[0][:, 1, :], in_=z_v[0][:, 1, :])
+        nc.sync.dma_start(out=tf_sb[0][0][:, 0:2, :], in_=tf_v[0][:, 0:2, 0:512])
+        nc.sync.dma_start(out=z_sb[0][:, 2:4, :], in_=z_v[0][:, 2:4, :])
+        nc.sync.dma_start(out=tf_sb[0][0][:, 2:4, :], in_=tf_v[0][:, 2:4, 0:512])
+        nc.sync.dma_start(out=e_sb[:, 1024:4096].bitcast(I32), in_=e_words[0][:, 1024:4096].bitcast(I32))
+        for c in range(1, NC):
+            nc.sync.dma_start(out=tf_sb[0][c][:], in_=tf_v[0][:, :, 512 * c : 512 * c + 512])
+        for h in range(2):
+            nc.sync.dma_start(out=q_sb[h][:], in_=q_v[h])
+        nc.sync.dma_start(out=z_sb[1][:], in_=z_v[1])
+        for c in range(NC):
+            nc.sync.dma_start(out=tf_sb[1][c][:], in_=tf_v[1][:, :, 512 * c : 512 * c + 512])
+
+        nc.scalar.activation(out=dummy[:], in_=dummy[:], func=ACT.Abs_reciprocal_sqrt)
+
+        def word_transposes(words, offsets):
+            bank = ps_a.tile([P, 4, P], F32, name="acc")
+            for i in range(2):
+                for u in range(2):
+                    nc.tensor.transpose(bank[:, 2 * i + u, :], words[:, offsets[i] + u : offsets[i] + 256 : 2], ident[:])
+            return bank
+
+        def word_copy(eng, bank, grouped, half):
+            dst = grouped[:, 256 * half : 256 * half + 256, :].rearrange("p (i r) t -> p i (r t)", i=2).bitcast(F32)
+            dst = dst.rearrange("p i (r u) -> p i r u", u=2)
+            srcv = bank[:].rearrange("p (i u) r -> p i r u", u=2)
+            if eng == "v":
+                nc.vector.tensor_copy(out=dst, in_=srcv)
+            else:
+                nc.scalar.copy(out=dst, in_=srcv)
+
+        def quant(codes, scales, grouped, lo, hi):
+            nc.vector.quantize_mx(
+                out=codes[:, lo:hi].bitcast(FP8X4),
+                scales=scales[:, lo:hi],
+                in_=grouped[:, lo:hi, :].rearrange("p w t -> p (w t)"),
+            )
+
+        def z_words(g):
+            return z_sb[g][:].rearrange("p s k -> p (s k)").bitcast(F32)
+
+        def for_constants():
+            nc.vector.tensor_scalar(out=nlen[:], in0=r_sb[:].rearrange("p g t -> p (g t)"), scalar1=0.75, scalar2=0.25, op0=ALU.mult, op1=ALU.add)
+            nc.vector.tensor_scalar(out=nlen2[:], in0=nlen[:], scalar1=1.2, scalar2=None, op0=ALU.mult)
+            nc.vector.reciprocal(out=invn[:], in_=nlen2[:])
+            nc.vector.tensor_scalar(out=sinv[:], in0=invn[:], scalar1=1.28, scalar2=None, op0=ALU.mult)
+            nc.vector.tensor_scalar(out=binv[:], in0=sinv[:], scalar1=-0.3, scalar2=1.28, op0=ALU.mult, op1=ALU.add)
+
+        for s in range(4):
+            zbank = ps_a.tile([P, 2, P], F32, name="acc")
+            for u in range(2):
+                nc.tensor.transpose(zbank[:, u, :], z_words(0)[:, 256 * s + u : 256 * s + 256 : 2], ident[:])
+            dst = zg[0][:, P * s : P * s + P, :].rearrange("p r t -> p (r t)").bitcast(F32).rearrange("p (r u) -> p r u", u=2)
+            if s % 2 == 0:
+                nc.vector.tensor_copy(out=dst, in_=zbank[:].rearrange("p u r -> p r u"))
+            else:
+                nc.scalar.copy(out=dst, in_=zbank[:].rearrange("p u r -> p r u"))
+            quant(zc[0], zs[0], zg[0], P * s, P * s + P)
+            if s == 0:
+                for_constants()
+
+        qg = [keep.tile([P, 512, 4], BF16, name="qg%d" % c, align_bytes=64) for c in range(NC)]
+        qc = [keep.tile([P, 512], U32, name="qc%d" % c, align_bytes=64) for c in range(NC)]
+        qs = [keep.tile([P, 512], U8, name="qs%d" % c, align_bytes=64) for c in range(NC)]
+        gc = [keep.tile([P, 512], U32, name="gc%d" % u, align_bytes=64) for u in range(NG * NC)]
+        gs = [keep.tile([P, 512], U8, name="gs%d" % u, align_bytes=64) for u in range(NG * NC)]
+
+        sim, tt, rr, yy, xx, gg = {}, {}, {}, {}, {}, {}
+
+        def mm1(j):
+            g, c, s = j // 16, (j % 16) // 4, j % 4
+            sim[j] = ps_s.tile([P, 512], F32, name="sim")
+            nc.tensor.matmul_mx(
+                out=sim[j][:],
+                lhsT=zc[g][:, P * s : P * s + P].bitcast(FP8X4),
+                lhsT_scale=zs[g][:, P * s : P * s + P],
+                rhs=e_sb[:, 1024 * c : 1024 * c + 1024].bitcast(FP4X4),
+                rhs_scale=es_sb[:, 512 * c : 512 * c + 512],
+                start=True,
+                stop=True,
+            )
+
+        def stt1(j):
+            g, c, s = j // 16, (j % 16) // 4, j % 4
+            tt[j] = work.tile([P, 4, P], F32, name="tt")
+            nc.vector.scalar_tensor_tensor(
+                out=tt[j][:],
+                in0=sim[j][:].rearrange("p (k t) -> p t k", t=4),
+                scalar=0.3,
+                in1=tf_sb[g][c][:, s, :].rearrange("p (k t) -> p t k", t=4),
+                op0=ALU.max,
+                op1=ALU.add,
+            )
+
+        def sq(j):
+            g, s = j // 16, j % 4
+            rr[j] = work.tile([P, 4, P], F32, name="rr")
+            nc.scalar.activation(out=rr[j][:], in_=tt[j][:], func=ACT.Square,
+                                 scale=sinv[:, 4 * g + s : 4 * g + s + 1], bias=binv[:, 4 * g + s : 4 * g + s + 1])
+
+        def ars(j):
+            yy[j] = work.tile([P, 4, P], F32, name="yy")
+            nc.scalar.activation(out=yy[j][:], in_=rr[j][:], func=ACT.Abs_reciprocal_sqrt)
+
+        def tr(j):
+            xx[j] = ps_x.tile([P, 4, P], F32, name="xx")
+            for t in range(4):
+                nc.tensor.transpose(xx[j][:, t, :], yy[j][:, t, :], ident[:])
+
+        def rd(j):
+            c, s, u = (j % 16) // 4, j % 4, j // 4
+            if s == 0:
+                gg[u] = work.tile([P, 512, 4], BF16, name="gg", align_bytes=64)
+            nc.vector.scalar_tensor_tensor(
+                out=gg[u][:, P * s : P * s + P, :],
+                in0=xx[j][:].rearrange("p t d -> p d t"),
+                scalar=0.78125,
+                in1=idfn[:, c, :].unsqueeze(1).to_broadcast([P, P, 4]),
+                op0=ALU.subtract,
+                op1=ALU.mult,
+            )
+
+        acc, osb, tb = {}, {}, {}
+        pg = [keep.tile([P, 512, 4], BF16, name="pg%d" % g, align_bytes=64) for g in range(NG)]
+        pc = [keep.tile([P, 512], U32, name="pc%d" % g, align_bytes=64) for g in range(NG)]
+        pss = [keep.tile([P, 512], U8, name="pss%d" % g, align_bytes=64) for g in range(NG)]
+
+        def mm2(g, mt, c):
+            if c == 0:
+                acc[g, mt] = ps_a.tile([P, 512], F32, name="acc")
+            nc.tensor.matmul_mx(
+                out=acc[g, mt][:],
+                lhsT=qc[c][:, P * mt : P * mt + P].bitcast(FP8X4),
+                lhsT_scale=qs[c][:, P * mt : P * mt + P],
+                rhs=gc[NC * g + c][:].bitcast(FP8X4),
+                rhs_scale=gs[NC * g + c][:],
+                start=(c == 0),
+                stop=(c == NC - 1),
+            )
+
+        def out_copy(eng, g, mt):
+            osb[g, mt] = keep.tile([P, 512], F32, name="osb%d_%d" % (g, mt))
+            dst = osb[g, mt][:].rearrange("p (k t) -> p k t", t=4)
+            srcv = acc[g, mt][:].rearrange("p (t k) -> p k t", t=4)
+            if eng == "v":
+                nc.vector.tensor_copy(out=dst, in_=srcv)
+            else:
+                nc.scalar.copy(out=dst, in_=srcv)
+            nc.sync.dma_start(out=out_0[P * mt : P * mt + P, 512 * g : 512 * g + 512], in_=osb[g, mt][:])
+
+        def out_tr(g, mt, pool, name):
+            tb[g, mt] = pool.tile([P, 4, P], F32, name=name)
+            for t in range(4):
+                nc.tensor.transpose(tb[g, mt][:, t, :], osb[g, mt][:, t : 512 : 4], ident[:])
+
+        def p_copy(eng, g, mt):
+            dst = pg[g][:, P * mt : P * mt + P, :]
+            srcv = tb[g, mt][:].rearrange("p t m -> p m t")
+            if eng == "v":
+                nc.vector.tensor_copy(out=dst, in_=srcv)
+            else:
+                nc.scalar.copy(out=dst, in_=srcv)
+
+        def p_quant(g, lo, hi):
+            quant(pc[g], pss[g], pg[g], lo, hi)
+            nc.sync.dma_start(
+                out=out_1[g].rearrange("p m t -> p (m t)")[:, 4 * lo : 4 * hi].bitcast(I32),
+                in_=pc[g][:, lo:hi].bitcast(I32),
+            )
+
+        def p_scales(g):
+            for qd in range(4):
+                eng = nc.sync if (qd % 2 == 0 or g == 0) else nc.scalar
+                eng.dma_start(
+                    out=out_2[g][4 * qd : 4 * qd + 4, :].bitcast(I32),
+                    in_=pss[g][32 * qd : 32 * qd + 4, :].bitcast(I32),
+                )
+
+        pe_x, act_x, vec_x = {}, {}, {}
+
+        def at(d, j, f):
+            d.setdefault(j, []).append(f)
+
+        banks = {}
+
+        def q_words(h):
+            return q_sb[h][:].rearrange("p t v -> p (t v)").bitcast(F32)
+
+        def q_tr(c, h):
+            banks["q", c, h] = word_transposes(q_words(h), [256 * c, 1024 + 256 * c])
+
+        def z_tr(h):
+            banks["z", h] = word_transposes(z_words(1), [512 * h, 512 * h + 256])
+
+        j = 3
+        for kind in ("q0", "q1", "z1", "q2", "q3"):
+            for h in range(2):
+                if kind == "z1":
+                    at(pe_x, j, lambda h=h: z_tr(h))
+                    at(act_x, j + 1, lambda h=h: word_copy("a", banks["z", h], zg[1], h))
+                else:
+                    c = int(kind[1])
+                    at(pe_x, j, lambda c=c, h=h: q_tr(c, h))
+                    at(act_x, j + 1, lambda c=c, h=h: word_copy("a", banks["q", c, h], qg[c], h))
+                j += 1
+            if kind == "z1":
+                at(vec_x, j + 1, lambda: quant(zc[1], zs[1], zg[1], 0, 512))
+            else:
+                c = int(kind[1])
+                at(vec_x, j + 1, lambda c=c: quant(qc[c], qs[c], qg[c], 0, 512))
+        for u in range(NG * NC):
+            if u < NG * NC - 1:
+                at(vec_x, 4 * u + 6, lambda u=u: quant(gc[u], gs[u], gg[u], 0, 512))
+            else:
+                at(vec_x, 4 * u + 4, lambda u=u: quant(gc[u], gs[u], gg[u], 0, 256))
+                at(vec_x, 4 * u + 6, lambda u=u: quant(gc[u], gs[u], gg[u], 256, 512))
+        obf = [keep.tile([P, 2, 512], BF16, name="obf%d" % h) for h in range(2)]
+
+        def o_round(mt):
+            nc.gpsimd.tensor_scalar(out=obf[mt // 2][:, mt % 2, :], in0=osb[0, mt][:], scalar1=1.0, scalar2=0.0, op0=ALU.mult, op1=ALU.add)
+
+        def o_tr(h):
+            banks["o", h] = word_transposes(obf[h][:].rearrange("p i n -> p (i n)").bitcast(F32), [0, 256])
+
+        for mt in range(4):
+            b = 19 + 2 * mt
+            for c in range(4):
+                at(pe_x, b + c // 2, lambda mt=mt, c=c: mm2(0, mt, c))
+            at(act_x, b + 2, lambda mt=mt: out_copy("a", 0, mt))
+            at(act_x, b + 2, lambda mt=mt: o_round(mt))
+        for h in range(2):
+            at(pe_x, 25 + 4 * h, lambda h=h: o_tr(h))
+            at(act_x, 26 + 4 * h, lambda h=h: word_copy("a", banks["o", h], pg[0], h))
+        at(vec_x, 31, lambda: p_quant(0, 0, 512))
+        at(vec_x, 31, lambda: p_scales(0))
+        for mt in range(4):
+            for c in range(2):
+                at(pe_x, 27 + mt, lambda mt=mt, c=c: mm2(1, mt, c))
+            at(pe_x, 31 + mt // 2, lambda mt=mt: mm2(1, mt, 2))
+
+        mm1(0)
+        for j in range(BLOCKS + 4):
+            if j < BLOCKS:
+                stt1(j)
+            if j == 1:
+                nc.vector.tensor_scalar(out=idfn[:].rearrange("p c t -> p (c t)"), in0=idf_sb[:].rearrange("p c t -> p (c t)"), scalar1=-2.2 * 1.28, scalar2=None, op0=ALU.mult)
+            if 0 <= j - 1 < BLOCKS:
+                ars(j - 1)
+            if j + 1 < BLOCKS:
+                mm1(j + 1)
+            if j < BLOCKS:
+                sq(j)
+            if 0 <= j - 1 < BLOCKS:
+                tr(j - 1)
+            for f in pe_x.get(j, []):
+                f()
+            for f in vec_x.get(j, []):
+                f()
+            if 0 <= j - 2 < BLOCKS:
+                rd(j - 2)
+            for f in act_x.get(j, []):
+                f()
+
+        for mt in range(4):
+            mm2(1, mt, 3)
+        for mt in range(4):
+            out_copy("av"[mt % 2], 1, mt)
+        for mt in range(4):
+            if mt % 2 == 0:
+                out_tr(1, mt, ps_s, "sim")
+            else:
+                out_tr(1, mt, ps_x, "xx")
+            p_copy("av"[mt % 2], 1, mt)
+            if mt % 2 == 1:
+                p_quant(1, 128 * (mt - 1), 128 * (mt + 1))
+        p_scales(1)

@@ -21,13 +21,20 @@ G_DOCS = 512
 NG = N // G_DOCS
 NC = V // 512
 BLOCKS = NG * NC * 4
+QD = 1
+A_INV = 77.0 / 128.0
+A_SCALE = 128.0 / 77.0
+U_PAIRS = set([])
+U_BLOCKS = set([2 * k + 1 for k in U_PAIRS])
+POOL_SQ = set([2 * k if k in U_PAIRS else 2 * k + 1 for k in range(15)])
 
 
 def tile_embeddingthresholdexpandedbm25scores_x2_kernel(tc, tf, z, e_words, e_scales, r, idf, q, out_0, out_1, out_2):
     nc = tc.nc
     with ExitStack() as ctx:
         keep = ctx.enter_context(tc.tile_pool(name="keep", bufs=1))
-        work = ctx.enter_context(tc.tile_pool(name="work", bufs=3))
+        gpool = ctx.enter_context(tc.tile_pool(name="gpool", bufs=3))
+        work = ctx.enter_context(tc.tile_pool(name="work", bufs=4))
         ps_s = ctx.enter_context(tc.psum_pool(name="ps_s", bufs=2))
         ps_x = ctx.enter_context(tc.psum_pool(name="ps_x", bufs=2))
         ps_a = ctx.enter_context(tc.psum_pool(name="ps_a", bufs=4))
@@ -78,18 +85,19 @@ def tile_embeddingthresholdexpandedbm25scores_x2_kernel(tc, tf, z, e_words, e_sc
         nc.sync.dma_start(out=z_sb[0][:, 2:4, :], in_=z_v[0][:, 2:4, :])
         nc.sync.dma_start(out=tf_sb[0][0][:, 2:4, :], in_=tf_v[0][:, 2:4, 0:512])
         nc.sync.dma_start(out=e_sb[:, 1024:4096].bitcast(I32), in_=e_words[0][:, 1024:4096].bitcast(I32))
-        for c in range(1, NC):
-            nc.sync.dma_start(out=tf_sb[0][c][:], in_=tf_v[0][:, :, 512 * c : 512 * c + 512])
-        for h in range(2):
-            nc.sync.dma_start(out=q_sb[h][:], in_=q_v[h])
+        nc.sync.dma_start(out=tf_sb[0][1][:], in_=tf_v[0][:, :, 512:1024])
         nc.sync.dma_start(out=z_sb[1][:], in_=z_v[1])
+        nc.sync.dma_start(out=tf_sb[0][2][:], in_=tf_v[0][:, :, 1024:1536])
+        nc.sync.dma_start(out=q_sb[0][:], in_=q_v[0])
+        nc.sync.dma_start(out=q_sb[1][:], in_=q_v[1])
+        nc.sync.dma_start(out=tf_sb[0][3][:], in_=tf_v[0][:, :, 1536:2048])
         for c in range(NC):
             nc.sync.dma_start(out=tf_sb[1][c][:], in_=tf_v[1][:, :, 512 * c : 512 * c + 512])
 
         nc.scalar.activation(out=dummy[:], in_=dummy[:], func=ACT.Abs_reciprocal_sqrt)
 
-        def word_transposes(words, offsets):
-            bank = ps_a.tile([P, 4, P], F32, name="acc")
+        def word_transposes(words, offsets, pool=ps_a, name="acc"):
+            bank = pool.tile([P, 4, P], F32, name=name)
             for i in range(2):
                 for u in range(2):
                     nc.tensor.transpose(bank[:, 2 * i + u, :], words[:, offsets[i] + u : offsets[i] + 256 : 2], ident[:])
@@ -118,21 +126,8 @@ def tile_embeddingthresholdexpandedbm25scores_x2_kernel(tc, tf, z, e_words, e_sc
             nc.vector.tensor_scalar(out=nlen[:], in0=r_sb[:].rearrange("p g t -> p (g t)"), scalar1=0.75, scalar2=0.25, op0=ALU.mult, op1=ALU.add)
             nc.vector.tensor_scalar(out=nlen2[:], in0=nlen[:], scalar1=1.2, scalar2=None, op0=ALU.mult)
             nc.vector.reciprocal(out=invn[:], in_=nlen2[:])
-            nc.vector.tensor_scalar(out=sinv[:], in0=invn[:], scalar1=1.28, scalar2=None, op0=ALU.mult)
-            nc.vector.tensor_scalar(out=binv[:], in0=sinv[:], scalar1=-0.3, scalar2=1.28, op0=ALU.mult, op1=ALU.add)
-
-        for s in range(4):
-            zbank = ps_a.tile([P, 2, P], F32, name="acc")
-            for u in range(2):
-                nc.tensor.transpose(zbank[:, u, :], z_words(0)[:, 256 * s + u : 256 * s + 256 : 2], ident[:])
-            dst = zg[0][:, P * s : P * s + P, :].rearrange("p r t -> p (r t)").bitcast(F32).rearrange("p (r u) -> p r u", u=2)
-            if s % 2 == 0:
-                nc.vector.tensor_copy(out=dst, in_=zbank[:].rearrange("p u r -> p r u"))
-            else:
-                nc.scalar.copy(out=dst, in_=zbank[:].rearrange("p u r -> p r u"))
-            quant(zc[0], zs[0], zg[0], P * s, P * s + P)
-            if s == 0:
-                for_constants()
+            nc.vector.tensor_scalar(out=sinv[:], in0=invn[:], scalar1=A_SCALE, scalar2=None, op0=ALU.mult)
+            nc.vector.tensor_scalar(out=binv[:], in0=sinv[:], scalar1=-0.3, scalar2=A_SCALE, op0=ALU.mult, op1=ALU.add)
 
         qg = [keep.tile([P, 512, 4], BF16, name="qg%d" % c, align_bytes=64) for c in range(NC)]
         qc = [keep.tile([P, 512], U32, name="qc%d" % c, align_bytes=64) for c in range(NC)]
@@ -155,45 +150,57 @@ def tile_embeddingthresholdexpandedbm25scores_x2_kernel(tc, tf, z, e_words, e_sc
                 stop=True,
             )
 
-        def stt1(j):
+        def tf_view(j):
             g, c, s = j // 16, (j % 16) // 4, j % 4
-            tt[j] = work.tile([P, 4, P], F32, name="tt")
-            nc.vector.scalar_tensor_tensor(
-                out=tt[j][:],
-                in0=sim[j][:].rearrange("p (k t) -> p t k", t=4),
-                scalar=0.3,
-                in1=tf_sb[g][c][:, s, :].rearrange("p (k t) -> p t k", t=4),
-                op0=ALU.max,
-                op1=ALU.add,
-            )
+            return tf_sb[g][c][:, s, :].rearrange("p (k t) -> p t k", t=4)
+
+        uu = {}
+
+        def relu(j):
+            if j in U_BLOCKS:
+                uu[j] = work.tile([P, 4, P], F32, name="uu")
+                nc.scalar.activation(out=uu[j][:], in_=sim[j][:].rearrange("p (k t) -> p t k", t=4), func=ACT.Relu, bias=-0.3)
+                tt[j] = work.tile([P, 4, P], F32, name="tt")
+                nc.gpsimd.tensor_tensor(out=tt[j][:], in0=uu[j][:], in1=tf_view(j), op=ALU.add)
+
+        def stt1(j):
+            if j not in U_BLOCKS:
+                tt[j] = work.tile([P, 4, P], F32, name="tt")
+                nc.vector.scalar_tensor_tensor(out=tt[j][:], in0=sim[j][:].rearrange("p (k t) -> p t k", t=4), scalar=0.3,
+                                               in1=tf_view(j), op0=ALU.max, op1=ALU.add)
 
         def sq(j):
             g, s = j // 16, j % 4
             rr[j] = work.tile([P, 4, P], F32, name="rr")
-            nc.scalar.activation(out=rr[j][:], in_=tt[j][:], func=ACT.Square,
-                                 scale=sinv[:, 4 * g + s : 4 * g + s + 1], bias=binv[:, 4 * g + s : 4 * g + s + 1])
+            sl = 4 * g + s
+            if j in POOL_SQ:
+                nc.scalar.activation(out=rr[j][:], in_=tt[j][:], func=ACT.Abs_reciprocal_sqrt,
+                                     scale=sinv[:, sl : sl + 1], bias=binv[:, sl : sl + 1])
+            else:
+                nc.scalar.activation(out=rr[j][:], in_=tt[j][:], func=ACT.Square, scale=sinv[:, sl : sl + 1],
+                                     bias=A_SCALE if j in U_BLOCKS else binv[:, sl : sl + 1])
 
         def ars(j):
             yy[j] = work.tile([P, 4, P], F32, name="yy")
-            nc.scalar.activation(out=yy[j][:], in_=rr[j][:], func=ACT.Abs_reciprocal_sqrt)
+            if j in POOL_SQ:
+                nc.gpsimd.tensor_tensor(out=yy[j][:], in0=rr[j][:], in1=rr[j][:], op=ALU.mult)
+            else:
+                nc.scalar.activation(out=yy[j][:], in_=rr[j][:], func=ACT.Abs_reciprocal_sqrt)
 
         def tr(j):
             xx[j] = ps_x.tile([P, 4, P], F32, name="xx")
             for t in range(4):
                 nc.tensor.transpose(xx[j][:, t, :], yy[j][:, t, :], ident[:])
 
+        def grouped(j):
+            u, s = j // 4, j % 4
+            if u not in gg:
+                gg[u] = gpool.tile([P, 512, 4], BF16, name="gg", align_bytes=64)
+            return gg[u][:, P * s : P * s + P, :]
+
         def rd(j):
-            c, s, u = (j % 16) // 4, j % 4, j // 4
-            if s == 0:
-                gg[u] = work.tile([P, 512, 4], BF16, name="gg", align_bytes=64)
-            nc.vector.scalar_tensor_tensor(
-                out=gg[u][:, P * s : P * s + P, :],
-                in0=xx[j][:].rearrange("p t d -> p d t"),
-                scalar=0.78125,
-                in1=idfn[:, c, :].unsqueeze(1).to_broadcast([P, P, 4]),
-                op0=ALU.subtract,
-                op1=ALU.mult,
-            )
+            nc.vector.scalar_tensor_tensor(out=grouped(j), in0=xx[j][:].rearrange("p t d -> p d t"), scalar=A_INV,
+                                           in1=idfn[:, (j % 16) // 4, :].unsqueeze(1).to_broadcast([P, P, 4]), op0=ALU.subtract, op1=ALU.mult)
 
         acc, osb, tb = {}, {}, {}
         pg = [keep.tile([P, 512, 4], BF16, name="pg%d" % g, align_bytes=64) for g in range(NG)]
@@ -267,77 +274,107 @@ def tile_embeddingthresholdexpandedbm25scores_x2_kernel(tc, tf, z, e_words, e_sc
         def z_tr(h):
             banks["z", h] = word_transposes(z_words(1), [512 * h, 512 * h + 256])
 
-        j = 3
-        for kind in ("q0", "q1", "z1", "q2", "q3"):
-            for h in range(2):
-                if kind == "z1":
-                    at(pe_x, j, lambda h=h: z_tr(h))
-                    at(act_x, j + 1, lambda h=h: word_copy("a", banks["z", h], zg[1], h))
-                else:
-                    c = int(kind[1])
-                    at(pe_x, j, lambda c=c, h=h: q_tr(c, h))
-                    at(act_x, j + 1, lambda c=c, h=h: word_copy("a", banks["q", c, h], qg[c], h))
-                j += 1
-            if kind == "z1":
-                at(vec_x, j + 1, lambda: quant(zc[1], zs[1], zg[1], 0, 512))
-            else:
-                c = int(kind[1])
-                at(vec_x, j + 1, lambda c=c: quant(qc[c], qs[c], qg[c], 0, 512))
-        for u in range(NG * NC):
-            if u < NG * NC - 1:
-                at(vec_x, 4 * u + 6, lambda u=u: quant(gc[u], gs[u], gg[u], 0, 512))
-            else:
-                at(vec_x, 4 * u + 4, lambda u=u: quant(gc[u], gs[u], gg[u], 0, 256))
-                at(vec_x, 4 * u + 6, lambda u=u: quant(gc[u], gs[u], gg[u], 256, 512))
         obf = [keep.tile([P, 2, 512], BF16, name="obf%d" % h) for h in range(2)]
 
         def o_round(mt):
             nc.gpsimd.tensor_scalar(out=obf[mt // 2][:, mt % 2, :], in0=osb[0, mt][:], scalar1=1.0, scalar2=0.0, op0=ALU.mult, op1=ALU.add)
 
-        def o_tr(h):
-            banks["o", h] = word_transposes(obf[h][:].rearrange("p i n -> p (i n)").bitcast(F32), [0, 256])
+        def o_tr(h, pool, name):
+            banks["o", h] = word_transposes(obf[h][:].rearrange("p i n -> p (i n)").bitcast(F32), [0, 256], pool, name)
 
+        tr_x, mm_x = {}, {}
+        for k, kind, h in ((1, "z", 0), (2, "z", 1), (3, "q0", 0), (3, "q0", 1), (4, "q1", 0), (5, "q1", 1), (5, "q2", 0), (6, "q2", 1), (7, "q3", 0), (8, "q3", 1)):
+            if kind == "z":
+                at(tr_x, k, lambda h=h: z_tr(h))
+                at(act_x, k, lambda h=h: word_copy("a", banks["z", h], zg[1], h))
+                if h == 1:
+                    at(vec_x, k + 1, lambda: quant(zc[1], zs[1], zg[1], 0, 512))
+            else:
+                c = int(kind[1])
+                at(tr_x, k, lambda c=c, h=h: q_tr(c, h))
+                at(act_x, k, lambda c=c, h=h: word_copy("a", banks["q", c, h], qg[c], h))
+                if h == 1:
+                    at(vec_x, k + QD, lambda c=c: quant(qc[c], qs[c], qg[c], 0, 512))
+        for u in range(NG * NC - 1):
+            at(vec_x, 2 * u + 3, lambda u=u: quant(gc[u], gs[u], gg[u], 0, 512))
         for mt in range(4):
-            b = 19 + 2 * mt
             for c in range(4):
-                at(pe_x, b + c // 2, lambda mt=mt, c=c: mm2(0, mt, c))
-            at(act_x, b + 2, lambda mt=mt: out_copy("a", 0, mt))
-            at(act_x, b + 2, lambda mt=mt: o_round(mt))
-        for h in range(2):
-            at(pe_x, 25 + 4 * h, lambda h=h: o_tr(h))
-            at(act_x, 26 + 4 * h, lambda h=h: word_copy("a", banks["o", h], pg[0], h))
-        at(vec_x, 31, lambda: p_quant(0, 0, 512))
-        at(vec_x, 31, lambda: p_scales(0))
-        for mt in range(4):
-            for c in range(2):
-                at(pe_x, 27 + mt, lambda mt=mt, c=c: mm2(1, mt, c))
-            at(pe_x, 31 + mt // 2, lambda mt=mt: mm2(1, mt, 2))
+                at(mm_x, 9 + mt, lambda mt=mt, c=c: mm2(0, mt, c))
+            at(act_x, 10 + mt, lambda mt=mt: out_copy("a", 0, mt))
+            at(act_x, 10 + mt, lambda mt=mt: o_round(mt))
+        at(tr_x, 13, lambda: o_tr(0, ps_a, "acc"))
+        at(act_x, 14, lambda: word_copy("a", banks["o", 0], pg[0], 0))
+        for k, mt, c in ((13, 0, 0), (13, 0, 1), (13, 1, 0), (13, 1, 1), (14, 2, 0), (14, 2, 1), (15, 3, 0), (15, 3, 1), (15, 0, 2), (15, 1, 2), (16, 2, 2), (16, 3, 2)):
+            at(mm_x, k, lambda mt=mt, c=c: mm2(1, mt, c))
 
+        PAIRS = BLOCKS // 2
+        for_constants()
+
+        def z0(s, eng):
+            zbank = ps_a.tile([P, 2, P], F32, name="acc")
+            for u in range(2):
+                nc.tensor.transpose(zbank[:, u, :], z_words(0)[:, 256 * s + u : 256 * s + 256 : 2], ident[:])
+            dst = zg[0][:, P * s : P * s + P, :].rearrange("p r t -> p (r t)").bitcast(F32).rearrange("p (r u) -> p r u", u=2)
+            if eng == "v":
+                nc.vector.tensor_copy(out=dst, in_=zbank[:].rearrange("p u r -> p r u"))
+            else:
+                nc.scalar.copy(out=dst, in_=zbank[:].rearrange("p u r -> p r u"))
+
+        z0(0, "v")
+        z0(1, "a")
+        quant(zc[0], zs[0], zg[0], 0, P)
         mm1(0)
-        for j in range(BLOCKS + 4):
-            if j < BLOCKS:
-                stt1(j)
-            if j == 1:
-                nc.vector.tensor_scalar(out=idfn[:].rearrange("p c t -> p (c t)"), in0=idf_sb[:].rearrange("p c t -> p (c t)"), scalar1=-2.2 * 1.28, scalar2=None, op0=ALU.mult)
-            if 0 <= j - 1 < BLOCKS:
-                ars(j - 1)
-            if j + 1 < BLOCKS:
-                mm1(j + 1)
-            if j < BLOCKS:
-                sq(j)
-            if 0 <= j - 1 < BLOCKS:
-                tr(j - 1)
-            for f in pe_x.get(j, []):
+        quant(zc[0], zs[0], zg[0], P, 2 * P)
+        mm1(1)
+        z0(2, "a")
+        z0(3, "a")
+        for k in range(PAIRS + 1):
+            if k < PAIRS:
+                stt1(2 * k)
+                if k == 0:
+                    quant(zc[0], zs[0], zg[0], 2 * P, 4 * P)
+                stt1(2 * k + 1)
+            if k == 0:
+                nc.vector.tensor_scalar(out=idfn[:].rearrange("p c t -> p (c t)"), in0=idf_sb[:].rearrange("p c t -> p (c t)"), scalar1=-2.2 * A_SCALE, scalar2=None, op0=ALU.mult)
+            if k < PAIRS - 1:
+                sq(2 * k)
+                sq(2 * k + 1)
+            if k == PAIRS - 1:
+                sq(2 * k)
+                ars(2 * k)
+                sq(2 * k + 1)
+                ars(2 * k + 1)
+            if k > 0:
+                tr(2 * k - 2)
+                tr(2 * k - 1)
+            for f in tr_x.get(k, []):
                 f()
-            for f in vec_x.get(j, []):
+            if k + 1 < PAIRS:
+                mm1(2 * k + 2)
+                mm1(2 * k + 3)
+            for f in vec_x.get(k, []):
                 f()
-            if 0 <= j - 2 < BLOCKS:
-                rd(j - 2)
-            for f in act_x.get(j, []):
+            for f in mm_x.get(k, []):
                 f()
+            if k == PAIRS:
+                quant(gc[7], gs[7], gg[7], 0, 256)
+            if k < PAIRS - 1:
+                ars(2 * k)
+                ars(2 * k + 1)
+                relu(2 * k + 3)
+            if k > 0:
+                rd(2 * k - 2)
+                rd(2 * k - 1)
+            for f in act_x.get(k, []):
+                f()
+        o_tr(1, ps_s, "sim")
+        word_copy("a", banks["o", 1], pg[0], 1)
+        quant(gc[7], gs[7], gg[7], 256, 512)
 
         for mt in range(4):
             mm2(1, mt, 3)
+        p_quant(0, 0, 512)
+        p_scales(0)
         for mt in range(4):
             out_copy("av"[mt % 2], 1, mt)
         for mt in range(4):

@@ -24,9 +24,9 @@ BLOCKS = NG * NC * 4
 QD = 1
 A_INV = 77.0 / 128.0
 A_SCALE = 128.0 / 77.0
-U_PAIRS = set([])
-U_BLOCKS = set([2 * k + 1 for k in U_PAIRS])
-POOL_SQ = set([2 * k if k in U_PAIRS else 2 * k + 1 for k in range(15)])
+OC0 = 10
+MM_FIRST = 1
+POOL_SQ = set([])
 
 
 def tile_embeddingthresholdexpandedbm25scores_x2_kernel(tc, tf, z, e_words, e_scales, r, idf, q, out_0, out_1, out_2):
@@ -37,7 +37,8 @@ def tile_embeddingthresholdexpandedbm25scores_x2_kernel(tc, tf, z, e_words, e_sc
         work = ctx.enter_context(tc.tile_pool(name="work", bufs=4))
         ps_s = ctx.enter_context(tc.psum_pool(name="ps_s", bufs=2))
         ps_x = ctx.enter_context(tc.psum_pool(name="ps_x", bufs=2))
-        ps_a = ctx.enter_context(tc.psum_pool(name="ps_a", bufs=4))
+        ps_a = ctx.enter_context(tc.psum_pool(name="ps_a", bufs=3))
+        ps_e = ctx.enter_context(tc.psum_pool(name="ps_e", bufs=1))
         ctx.enter_context(tc.manual_schedule())
 
         z_sb = []
@@ -85,18 +86,24 @@ def tile_embeddingthresholdexpandedbm25scores_x2_kernel(tc, tf, z, e_words, e_sc
         nc.sync.dma_start(out=z_sb[0][:, 2:4, :], in_=z_v[0][:, 2:4, :])
         nc.sync.dma_start(out=tf_sb[0][0][:, 2:4, :], in_=tf_v[0][:, 2:4, 0:512])
         nc.sync.dma_start(out=e_sb[:, 1024:4096].bitcast(I32), in_=e_words[0][:, 1024:4096].bitcast(I32))
+        def load_q(c):
+            for h in range(2):
+                nc.sync.dma_start(out=q_sb[h][:, :, 512 * c : 512 * c + 512], in_=q_v[h][:, :, 512 * c : 512 * c + 512])
+
+        load_q(0)
         nc.sync.dma_start(out=tf_sb[0][1][:], in_=tf_v[0][:, :, 512:1024])
         nc.sync.dma_start(out=z_sb[1][:], in_=z_v[1])
+        load_q(1)
         nc.sync.dma_start(out=tf_sb[0][2][:], in_=tf_v[0][:, :, 1024:1536])
-        nc.sync.dma_start(out=q_sb[0][:], in_=q_v[0])
-        nc.sync.dma_start(out=q_sb[1][:], in_=q_v[1])
+        load_q(2)
         nc.sync.dma_start(out=tf_sb[0][3][:], in_=tf_v[0][:, :, 1536:2048])
+        load_q(3)
         for c in range(NC):
             nc.sync.dma_start(out=tf_sb[1][c][:], in_=tf_v[1][:, :, 512 * c : 512 * c + 512])
 
         nc.scalar.activation(out=dummy[:], in_=dummy[:], func=ACT.Abs_reciprocal_sqrt)
 
-        def word_transposes(words, offsets, pool=ps_a, name="acc"):
+        def word_transposes(words, offsets, pool=ps_e, name="ext"):
             bank = pool.tile([P, 4, P], F32, name=name)
             for i in range(2):
                 for u in range(2):
@@ -121,13 +128,6 @@ def tile_embeddingthresholdexpandedbm25scores_x2_kernel(tc, tf, z, e_words, e_sc
 
         def z_words(g):
             return z_sb[g][:].rearrange("p s k -> p (s k)").bitcast(F32)
-
-        def for_constants():
-            nc.vector.tensor_scalar(out=nlen[:], in0=r_sb[:].rearrange("p g t -> p (g t)"), scalar1=0.75, scalar2=0.25, op0=ALU.mult, op1=ALU.add)
-            nc.vector.tensor_scalar(out=nlen2[:], in0=nlen[:], scalar1=1.2, scalar2=None, op0=ALU.mult)
-            nc.vector.reciprocal(out=invn[:], in_=nlen2[:])
-            nc.vector.tensor_scalar(out=sinv[:], in0=invn[:], scalar1=A_SCALE, scalar2=None, op0=ALU.mult)
-            nc.vector.tensor_scalar(out=binv[:], in0=sinv[:], scalar1=-0.3, scalar2=A_SCALE, op0=ALU.mult, op1=ALU.add)
 
         qg = [keep.tile([P, 512, 4], BF16, name="qg%d" % c, align_bytes=64) for c in range(NC)]
         qc = [keep.tile([P, 512], U32, name="qc%d" % c, align_bytes=64) for c in range(NC)]
@@ -154,20 +154,10 @@ def tile_embeddingthresholdexpandedbm25scores_x2_kernel(tc, tf, z, e_words, e_sc
             g, c, s = j // 16, (j % 16) // 4, j % 4
             return tf_sb[g][c][:, s, :].rearrange("p (k t) -> p t k", t=4)
 
-        uu = {}
-
-        def relu(j):
-            if j in U_BLOCKS:
-                uu[j] = work.tile([P, 4, P], F32, name="uu")
-                nc.scalar.activation(out=uu[j][:], in_=sim[j][:].rearrange("p (k t) -> p t k", t=4), func=ACT.Relu, bias=-0.3)
-                tt[j] = work.tile([P, 4, P], F32, name="tt")
-                nc.gpsimd.tensor_tensor(out=tt[j][:], in0=uu[j][:], in1=tf_view(j), op=ALU.add)
-
         def stt1(j):
-            if j not in U_BLOCKS:
-                tt[j] = work.tile([P, 4, P], F32, name="tt")
-                nc.vector.scalar_tensor_tensor(out=tt[j][:], in0=sim[j][:].rearrange("p (k t) -> p t k", t=4), scalar=0.3,
-                                               in1=tf_view(j), op0=ALU.max, op1=ALU.add)
+            tt[j] = work.tile([P, 4, P], F32, name="tt")
+            nc.vector.scalar_tensor_tensor(out=tt[j][:], in0=sim[j][:].rearrange("p (k t) -> p t k", t=4), scalar=0.3,
+                                           in1=tf_view(j), op0=ALU.max, op1=ALU.add)
 
         def sq(j):
             g, s = j // 16, j % 4
@@ -178,7 +168,7 @@ def tile_embeddingthresholdexpandedbm25scores_x2_kernel(tc, tf, z, e_words, e_sc
                                      scale=sinv[:, sl : sl + 1], bias=binv[:, sl : sl + 1])
             else:
                 nc.scalar.activation(out=rr[j][:], in_=tt[j][:], func=ACT.Square, scale=sinv[:, sl : sl + 1],
-                                     bias=A_SCALE if j in U_BLOCKS else binv[:, sl : sl + 1])
+                                     bias=binv[:, sl : sl + 1])
 
         def ars(j):
             yy[j] = work.tile([P, 4, P], F32, name="yy")
@@ -209,7 +199,7 @@ def tile_embeddingthresholdexpandedbm25scores_x2_kernel(tc, tf, z, e_words, e_sc
 
         def mm2(g, mt, c):
             if c == 0:
-                acc[g, mt] = ps_a.tile([P, 512], F32, name="acc")
+                acc[g, mt] = ps_e.tile([P, 512], F32, name="ext") if mt == 3 else ps_a.tile([P, 512], F32, name="acc")
             nc.tensor.matmul_mx(
                 out=acc[g, mt][:],
                 lhsT=qc[c][:, P * mt : P * mt + P].bitcast(FP8X4),
@@ -283,7 +273,7 @@ def tile_embeddingthresholdexpandedbm25scores_x2_kernel(tc, tf, z, e_words, e_sc
             banks["o", h] = word_transposes(obf[h][:].rearrange("p i n -> p (i n)").bitcast(F32), [0, 256], pool, name)
 
         tr_x, mm_x = {}, {}
-        for k, kind, h in ((1, "z", 0), (2, "z", 1), (3, "q0", 0), (3, "q0", 1), (4, "q1", 0), (5, "q1", 1), (5, "q2", 0), (6, "q2", 1), (7, "q3", 0), (8, "q3", 1)):
+        for k, (kind, h) in enumerate((kind, h) for kind in ("q0", "z", "q1", "q2", "q3") for h in range(2)):
             if kind == "z":
                 at(tr_x, k, lambda h=h: z_tr(h))
                 at(act_x, k, lambda h=h: word_copy("a", banks["z", h], zg[1], h))
@@ -294,24 +284,35 @@ def tile_embeddingthresholdexpandedbm25scores_x2_kernel(tc, tf, z, e_words, e_sc
                 at(tr_x, k, lambda c=c, h=h: q_tr(c, h))
                 at(act_x, k, lambda c=c, h=h: word_copy("a", banks["q", c, h], qg[c], h))
                 if h == 1:
-                    at(vec_x, k + QD, lambda c=c: quant(qc[c], qs[c], qg[c], 0, 512))
+                    at(vec_x, k + 1, lambda c=c: quant(qc[c], qs[c], qg[c], 0, 512))
         for u in range(NG * NC - 1):
             at(vec_x, 2 * u + 3, lambda u=u: quant(gc[u], gs[u], gg[u], 0, 512))
+        for k, g, mt, c in (
+            (3, 0, 0, 0), (3, 0, 1, 0), (4, 0, 2, 0), (6, 0, 0, 1), (7, 0, 1, 1), (7, 0, 2, 1), (8, 0, 0, 2), (8, 0, 1, 2), (9, 0, 2, 2),
+            (10, 0, 0, 3), (10, 0, 1, 3), (10, 0, 2, 3), (11, 0, 3, 0), (11, 0, 3, 1), (11, 0, 3, 2), (11, 0, 3, 3),
+            (12, 1, 0, 0), (12, 1, 1, 0), (13, 1, 0, 1), (13, 1, 1, 1), (13, 1, 2, 0), (14, 1, 2, 1),
+            (15, 1, 0, 2), (15, 1, 1, 2), (15, 1, 2, 2), (16, 1, 3, 0), (16, 1, 3, 1), (16, 1, 3, 2),
+        ):
+            at(mm_x, k, lambda g=g, mt=mt, c=c: mm2(g, mt, c))
         for mt in range(4):
-            for c in range(4):
-                at(mm_x, 9 + mt, lambda mt=mt, c=c: mm2(0, mt, c))
-            at(act_x, 10 + mt, lambda mt=mt: out_copy("a", 0, mt))
-            at(act_x, 10 + mt, lambda mt=mt: o_round(mt))
-        at(tr_x, 13, lambda: o_tr(0, ps_a, "acc"))
-        at(act_x, 14, lambda: word_copy("a", banks["o", 0], pg[0], 0))
-        for k, mt, c in ((13, 0, 0), (13, 0, 1), (13, 1, 0), (13, 1, 1), (14, 2, 0), (14, 2, 1), (15, 3, 0), (15, 3, 1), (15, 0, 2), (15, 1, 2), (16, 2, 2), (16, 3, 2)):
-            at(mm_x, k, lambda mt=mt, c=c: mm2(1, mt, c))
+            at(act_x, OC0 + mt, lambda mt=mt: out_copy("a", 0, mt))
+            at(act_x, OC0 + mt, lambda mt=mt: o_round(mt))
+        for h in range(2):
+            at(tr_x, 14 + h, lambda h=h: o_tr(h, ps_e, "ext"))
+            at(act_x, 14 + h, lambda h=h: word_copy("a", banks["o", h], pg[0], h))
 
         PAIRS = BLOCKS // 2
-        for_constants()
+        def const_ops():
+            return [
+                lambda: nc.vector.tensor_scalar(out=nlen[:], in0=r_sb[:].rearrange("p g t -> p (g t)"), scalar1=0.75, scalar2=0.25, op0=ALU.mult, op1=ALU.add),
+                lambda: nc.vector.tensor_scalar(out=nlen2[:], in0=nlen[:], scalar1=1.2, scalar2=None, op0=ALU.mult),
+                lambda: nc.vector.reciprocal(out=invn[:], in_=nlen2[:]),
+                lambda: nc.vector.tensor_scalar(out=sinv[:], in0=invn[:], scalar1=A_SCALE, scalar2=None, op0=ALU.mult),
+                lambda: nc.vector.tensor_scalar(out=binv[:], in0=sinv[:], scalar1=-0.3, scalar2=A_SCALE, op0=ALU.mult, op1=ALU.add),
+            ]
 
         def z0(s, eng):
-            zbank = ps_a.tile([P, 2, P], F32, name="acc")
+            zbank = ps_e.tile([P, 2, P], F32, name="ext") if s == 3 else ps_a.tile([P, 2, P], F32, name="acc")
             for u in range(2):
                 nc.tensor.transpose(zbank[:, u, :], z_words(0)[:, 256 * s + u : 256 * s + 256 : 2], ident[:])
             dst = zg[0][:, P * s : P * s + P, :].rearrange("p r t -> p (r t)").bitcast(F32).rearrange("p (r u) -> p r u", u=2)
@@ -320,36 +321,44 @@ def tile_embeddingthresholdexpandedbm25scores_x2_kernel(tc, tf, z, e_words, e_sc
             else:
                 nc.scalar.copy(out=dst, in_=zbank[:].rearrange("p u r -> p r u"))
 
+        cop = const_ops()
+        cop[0]()
         z0(0, "v")
+        cop[1]()
         z0(1, "a")
         quant(zc[0], zs[0], zg[0], 0, P)
+        cop[2]()
+        z0(2, "v")
+        z0(3, "a")
         mm1(0)
         quant(zc[0], zs[0], zg[0], P, 2 * P)
         mm1(1)
-        z0(2, "a")
-        z0(3, "a")
+        cop[3]()
+        quant(zc[0], zs[0], zg[0], 2 * P, 3 * P)
+        cop[4]()
+        quant(zc[0], zs[0], zg[0], 3 * P, 4 * P)
         for k in range(PAIRS + 1):
+            solo = k in (0, PAIRS - 1)
             if k < PAIRS:
                 stt1(2 * k)
-                if k == 0:
-                    quant(zc[0], zs[0], zg[0], 2 * P, 4 * P)
                 stt1(2 * k + 1)
+                sq(2 * k)
+                if solo:
+                    ars(2 * k)
+                sq(2 * k + 1)
+                if solo:
+                    ars(2 * k + 1)
             if k == 0:
                 nc.vector.tensor_scalar(out=idfn[:].rearrange("p c t -> p (c t)"), in0=idf_sb[:].rearrange("p c t -> p (c t)"), scalar1=-2.2 * A_SCALE, scalar2=None, op0=ALU.mult)
-            if k < PAIRS - 1:
-                sq(2 * k)
-                sq(2 * k + 1)
-            if k == PAIRS - 1:
-                sq(2 * k)
-                ars(2 * k)
-                sq(2 * k + 1)
-                ars(2 * k + 1)
+            if k < MM_FIRST:
+                mm1(2 * k + 2)
+                mm1(2 * k + 3)
             if k > 0:
                 tr(2 * k - 2)
                 tr(2 * k - 1)
             for f in tr_x.get(k, []):
                 f()
-            if k + 1 < PAIRS:
+            if MM_FIRST <= k < PAIRS - 1:
                 mm1(2 * k + 2)
                 mm1(2 * k + 3)
             for f in vec_x.get(k, []):
@@ -358,17 +367,14 @@ def tile_embeddingthresholdexpandedbm25scores_x2_kernel(tc, tf, z, e_words, e_sc
                 f()
             if k == PAIRS:
                 quant(gc[7], gs[7], gg[7], 0, 256)
-            if k < PAIRS - 1:
-                ars(2 * k)
-                ars(2 * k + 1)
-                relu(2 * k + 3)
             if k > 0:
                 rd(2 * k - 2)
                 rd(2 * k - 1)
+            if k < PAIRS and not solo:
+                ars(2 * k)
+                ars(2 * k + 1)
             for f in act_x.get(k, []):
                 f()
-        o_tr(1, ps_s, "sim")
-        word_copy("a", banks["o", 1], pg[0], 1)
         quant(gc[7], gs[7], gg[7], 256, 512)
 
         for mt in range(4):

@@ -26,7 +26,9 @@ A_INV = 77.0 / 128.0
 A_SCALE = 128.0 / 77.0
 OC0 = 10
 MM_FIRST = 1
-POOL_SQ = set([])
+EXT_LAST = set([1, 2, 3])
+Q0D = 1
+POOL_SQ = set([2 * k + 1 for k in range(1, 15)])
 
 
 def tile_embeddingthresholdexpandedbm25scores_x2_kernel(tc, tf, z, e_words, e_scales, r, idf, q, out_0, out_1, out_2):
@@ -51,8 +53,8 @@ def tile_embeddingthresholdexpandedbm25scores_x2_kernel(tc, tf, z, e_words, e_sc
             zg.append(keep.tile([P, 512, 4], BF16, name="zg%d" % g, align_bytes=64))
             zc.append(keep.tile([P, 512], U32, name="zc%d" % g, align_bytes=64))
             zs.append(keep.tile([P, 512], U8, name="zs%d" % g, align_bytes=64))
-        for h in range(2):
-            q_sb.append(keep.tile([P, 2, V], BF16, name="q_sb%d" % h, align_bytes=64))
+        for h in range(NC):
+            q_sb.append(keep.tile([P, 4, 512], BF16, name="q_sb%d" % h, align_bytes=64))
         e_sb = keep.tile([P, 2 * V], U8, name="e_sb", align_bytes=64)
         es_sb = keep.tile([P, V], U8, name="es_sb", align_bytes=64)
         ident = keep.tile([P, P], F32, name="ident")
@@ -68,29 +70,28 @@ def tile_embeddingthresholdexpandedbm25scores_x2_kernel(tc, tf, z, e_words, e_sc
 
         tf_v = tf.rearrange("(g p t) v -> g p t v", p=P, t=4)
         z_v = z.rearrange("(g p t) k -> g p t k", p=P, t=4)
-        q_v = q.rearrange("(h t p) v -> h p t v", p=P, t=2)
+        q_v = q.rearrange("(t p) v -> p t v", p=P)
         nc.vector.memset(dummy[:], 1.0)
         nc.vector.memset(es_sb[:].bitcast(I32), 0)
-        nc.scalar.dma_start(out=r_sb[:], in_=r.rearrange("(g p t) -> p g t", p=P, t=4))
         for qd in range(4):
             nc.scalar.dma_start(
                 out=es_sb[32 * qd : 32 * qd + 4, :].bitcast(I32),
                 in_=e_scales[0][4 * qd : 4 * qd + 4, :].bitcast(I32),
             )
-        nc.scalar.dma_start(out=idf_sb[:], in_=idf.rearrange("(c p t) -> p c t", p=P, t=4))
+        nc.gpsimd.dma_start(out=r_sb[:], in_=r.rearrange("(g p t) -> p g t", p=P, t=4))
         make_identity(nc, ident[:])
+        nc.gpsimd.dma_start(out=idf_sb[:], in_=idf.rearrange("(c p t) -> p c t", p=P, t=4))
+
+        def load_q(c):
+            nc.sync.dma_start(out=q_sb[c][:], in_=q_v[:, :, 512 * c : 512 * c + 512])
+
         nc.sync.dma_start(out=z_sb[0][:, 0, :], in_=z_v[0][:, 0, :])
         nc.sync.dma_start(out=e_sb[:, 0:1024].bitcast(I32), in_=e_words[0][:, 0:1024].bitcast(I32))
-        nc.sync.dma_start(out=z_sb[0][:, 1, :], in_=z_v[0][:, 1, :])
+        nc.sync.dma_start(out=z_sb[0][:, 1:4, :], in_=z_v[0][:, 1:4, :])
         nc.sync.dma_start(out=tf_sb[0][0][:, 0:2, :], in_=tf_v[0][:, 0:2, 0:512])
-        nc.sync.dma_start(out=z_sb[0][:, 2:4, :], in_=z_v[0][:, 2:4, :])
         nc.sync.dma_start(out=tf_sb[0][0][:, 2:4, :], in_=tf_v[0][:, 2:4, 0:512])
-        nc.sync.dma_start(out=e_sb[:, 1024:4096].bitcast(I32), in_=e_words[0][:, 1024:4096].bitcast(I32))
-        def load_q(c):
-            for h in range(2):
-                nc.sync.dma_start(out=q_sb[h][:, :, 512 * c : 512 * c + 512], in_=q_v[h][:, :, 512 * c : 512 * c + 512])
-
         load_q(0)
+        nc.sync.dma_start(out=e_sb[:, 1024:4096].bitcast(I32), in_=e_words[0][:, 1024:4096].bitcast(I32))
         nc.sync.dma_start(out=tf_sb[0][1][:], in_=tf_v[0][:, :, 512:1024])
         nc.sync.dma_start(out=z_sb[1][:], in_=z_v[1])
         load_q(1)
@@ -210,20 +211,29 @@ def tile_embeddingthresholdexpandedbm25scores_x2_kernel(tc, tf, z, e_words, e_sc
                 stop=(c == NC - 1),
             )
 
+        opair = {}
+
         def out_copy(eng, g, mt):
-            osb[g, mt] = keep.tile([P, 512], F32, name="osb%d_%d" % (g, mt))
-            dst = osb[g, mt][:].rearrange("p (k t) -> p k t", t=4)
+            if mt % 2 == 0:
+                opair[g, mt // 2] = keep.tile([P, 2, 512], F32, name="osb%d_%d" % (g, mt))
+            osb[g, mt] = opair[g, mt // 2][:, mt % 2, :]
+            dst = osb[g, mt].rearrange("p (k t) -> p k t", t=4)
             srcv = acc[g, mt][:].rearrange("p (t k) -> p k t", t=4)
             if eng == "v":
                 nc.vector.tensor_copy(out=dst, in_=srcv)
             else:
                 nc.scalar.copy(out=dst, in_=srcv)
-            nc.sync.dma_start(out=out_0[P * mt : P * mt + P, 512 * g : 512 * g + 512], in_=osb[g, mt][:])
+            if mt % 2 == 1:
+                h = mt // 2
+                nc.sync.dma_start(
+                    out=out_0[256 * h : 256 * h + 256, 512 * g : 512 * g + 512].rearrange("(i p) n -> p i n", p=P),
+                    in_=opair[g, h][:],
+                )
 
         def out_tr(g, mt, pool, name):
             tb[g, mt] = pool.tile([P, 4, P], F32, name=name)
             for t in range(4):
-                nc.tensor.transpose(tb[g, mt][:, t, :], osb[g, mt][:, t : 512 : 4], ident[:])
+                nc.tensor.transpose(tb[g, mt][:, t, :], osb[g, mt][:, t:512:4], ident[:])
 
         def p_copy(eng, g, mt):
             dst = pg[g][:, P * mt : P * mt + P, :]
@@ -255,11 +265,11 @@ def tile_embeddingthresholdexpandedbm25scores_x2_kernel(tc, tf, z, e_words, e_sc
 
         banks = {}
 
-        def q_words(h):
-            return q_sb[h][:].rearrange("p t v -> p (t v)").bitcast(F32)
+        def q_words(c):
+            return q_sb[c][:].rearrange("p t v -> p (t v)").bitcast(F32)
 
         def q_tr(c, h):
-            banks["q", c, h] = word_transposes(q_words(h), [256 * c, 1024 + 256 * c])
+            banks["q", c, h] = word_transposes(q_words(c), [512 * h, 512 * h + 256])
 
         def z_tr(h):
             banks["z", h] = word_transposes(z_words(1), [512 * h, 512 * h + 256])
@@ -267,7 +277,7 @@ def tile_embeddingthresholdexpandedbm25scores_x2_kernel(tc, tf, z, e_words, e_sc
         obf = [keep.tile([P, 2, 512], BF16, name="obf%d" % h) for h in range(2)]
 
         def o_round(mt):
-            nc.gpsimd.tensor_scalar(out=obf[mt // 2][:, mt % 2, :], in0=osb[0, mt][:], scalar1=1.0, scalar2=0.0, op0=ALU.mult, op1=ALU.add)
+            nc.gpsimd.tensor_scalar(out=obf[mt // 2][:, mt % 2, :], in0=osb[0, mt], scalar1=1.0, scalar2=0.0, op0=ALU.mult, op1=ALU.add)
 
         def o_tr(h, pool, name):
             banks["o", h] = word_transposes(obf[h][:].rearrange("p i n -> p (i n)").bitcast(F32), [0, 256], pool, name)
@@ -284,7 +294,7 @@ def tile_embeddingthresholdexpandedbm25scores_x2_kernel(tc, tf, z, e_words, e_sc
                 at(tr_x, k, lambda c=c, h=h: q_tr(c, h))
                 at(act_x, k, lambda c=c, h=h: word_copy("a", banks["q", c, h], qg[c], h))
                 if h == 1:
-                    at(vec_x, k + 1, lambda c=c: quant(qc[c], qs[c], qg[c], 0, 512))
+                    at(vec_x, k + (Q0D if c == 0 else 1), lambda c=c: quant(qc[c], qs[c], qg[c], 0, 512))
         for u in range(NG * NC - 1):
             at(vec_x, 2 * u + 3, lambda u=u: quant(gc[u], gs[u], gg[u], 0, 512))
         for k, g, mt, c in (
@@ -356,17 +366,23 @@ def tile_embeddingthresholdexpandedbm25scores_x2_kernel(tc, tf, z, e_words, e_sc
             if k > 0:
                 tr(2 * k - 2)
                 tr(2 * k - 1)
-            for f in tr_x.get(k, []):
-                f()
+            if k not in EXT_LAST:
+                for f in tr_x.get(k, []):
+                    f()
             if MM_FIRST <= k < PAIRS - 1:
                 mm1(2 * k + 2)
                 mm1(2 * k + 3)
+            if k in EXT_LAST:
+                for f in tr_x.get(k, []):
+                    f()
             for f in vec_x.get(k, []):
                 f()
             for f in mm_x.get(k, []):
                 f()
             if k == PAIRS:
                 quant(gc[7], gs[7], gg[7], 0, 256)
+                p_quant(0, 0, 512)
+                p_scales(0)
             if k > 0:
                 rd(2 * k - 2)
                 rd(2 * k - 1)
@@ -379,16 +395,14 @@ def tile_embeddingthresholdexpandedbm25scores_x2_kernel(tc, tf, z, e_words, e_sc
 
         for mt in range(4):
             mm2(1, mt, 3)
-        p_quant(0, 0, 512)
-        p_scales(0)
         for mt in range(4):
-            out_copy("av"[mt % 2], 1, mt)
+            out_copy("va"[mt % 2], 1, mt)
         for mt in range(4):
             if mt % 2 == 0:
                 out_tr(1, mt, ps_s, "sim")
             else:
                 out_tr(1, mt, ps_x, "xx")
-            p_copy("av"[mt % 2], 1, mt)
+            p_copy("va"[mt % 2], 1, mt)
             if mt % 2 == 1:
                 p_quant(1, 128 * (mt - 1), 128 * (mt + 1))
         p_scales(1)

from contextlib import ExitStack

import concourse.mybir as mybir
from concourse.masks import make_identity

N, V, D, M = 1024, 2048, 512, 512
FLOPS = 2 * N * D * V + 2 * M * V * N

F32 = mybir.dt.float32
BF16 = mybir.dt.bfloat16
U32 = mybir.dt.uint32
I32 = mybir.dt.int32
U8 = mybir.dt.uint8
FP8X4 = mybir.dt.float8_e4m3fn_x4
FP4X4 = mybir.dt.float4_e2m1fn_x4
ALU = mybir.AluOpType
ACT = mybir.ActivationFunctionType

P = 128
G_DOCS = 512
NG = N // G_DOCS
NC = V // 512
BLOCKS = NG * NC * 4
QD = 1
A_INV = 77.0 / 128.0
A_SCALE = 128.0 / 77.0
OC0 = 10
MM_FIRST = 1
EXT_LAST = set([1, 2, 3])
Q0D = 1
POOL_SQ = set([2 * k + 1 for k in range(1, 15)])


def tile_embeddingthresholdexpandedbm25scores_x2_kernel(tc, tf, z, e_words, e_scales, r, idf, q, out_0, out_1, out_2):
    nc = tc.nc
    with ExitStack() as ctx:
        keep = ctx.enter_context(tc.tile_pool(name="keep", bufs=1))
        gpool = ctx.enter_context(tc.tile_pool(name="gpool", bufs=3))
        work = ctx.enter_context(tc.tile_pool(name="work", bufs=4))
        ps_s = ctx.enter_context(tc.psum_pool(name="ps_s", bufs=2))
        ps_x = ctx.enter_context(tc.psum_pool(name="ps_x", bufs=2))
        ps_a = ctx.enter_context(tc.psum_pool(name="ps_a", bufs=3))
        ps_e = ctx.enter_context(tc.psum_pool(name="ps_e", bufs=1))
        ctx.enter_context(tc.manual_schedule())

        z_sb = []
        tf_sb = []
        q_sb = []
        zg, zc, zs = [], [], []
        for g in range(NG):
            z_sb.append(keep.tile([P, 4, D], BF16, name="z_sb%d" % g, align_bytes=64))
            tf_sb.append([keep.tile([P, 4, 512], BF16, name="tf%d_%d" % (g, c), align_bytes=64) for c in range(NC)])
            zg.append(keep.tile([P, 512, 4], BF16, name="zg%d" % g, align_bytes=64))
            zc.append(keep.tile([P, 512], U32, name="zc%d" % g, align_bytes=64))
            zs.append(keep.tile([P, 512], U8, name="zs%d" % g, align_bytes=64))
        for h in range(NC):
            q_sb.append(keep.tile([P, 4, 512], BF16, name="q_sb%d" % h, align_bytes=64))
        e_sb = keep.tile([P, 2 * V], U8, name="e_sb", align_bytes=64)
        es_sb = keep.tile([P, V], U8, name="es_sb", align_bytes=64)
        ident = keep.tile([P, P], F32, name="ident")
        r_sb = keep.tile([P, NG, 4], BF16, name="r_sb")
        idf_sb = keep.tile([P, NC, 4], BF16, name="idf_sb")
        dummy = keep.tile([P, 1], F32, name="dummy")
        nlen = keep.tile([P, NG * 4], F32, name="nlen")
        nlen2 = keep.tile([P, NG * 4], F32, name="nlen2")
        invn = keep.tile([P, NG * 4], F32, name="invn")
        sinv = keep.tile([P, NG * 4], F32, name="sinv")
        binv = keep.tile([P, NG * 4], F32, name="binv")
        idfn = keep.tile([P, NC, 4], F32, name="idfn")

        tf_v = tf.rearrange("(g p t) v -> g p t v", p=P, t=4)
        z_v = z.rearrange("(g p t) k -> g p t k", p=P, t=4)
        q_v = q.rearrange("(t p) v -> p t v", p=P)
        nc.vector.memset(dummy[:], 1.0)
        nc.vector.memset(es_sb[:].bitcast(I32), 0)
        for qd in range(4):
            nc.scalar.dma_start(
                out=es_sb[32 * qd : 32 * qd + 4, :].bitcast(I32),
                in_=e_scales[0][4 * qd : 4 * qd + 4, :].bitcast(I32),
            )
        nc.gpsimd.dma_start(out=r_sb[:], in_=r.rearrange("(g p t) -> p g t", p=P, t=4))
        make_identity(nc, ident[:])
        nc.gpsimd.dma_start(out=idf_sb[:], in_=idf.rearrange("(c p t) -> p c t", p=P, t=4))

        def load_q(c):
            nc.sync.dma_start(out=q_sb[c][:], in_=q_v[:, :, 512 * c : 512 * c + 512])

        nc.sync.dma_start(out=z_sb[0][:, 0, :], in_=z_v[0][:, 0, :])
        nc.sync.dma_start(out=e_sb[:, 0:1024].bitcast(I32), in_=e_words[0][:, 0:1024].bitcast(I32))
        nc.sync.dma_start(out=z_sb[0][:, 1:4, :], in_=z_v[0][:, 1:4, :])
        nc.sync.dma_start(out=tf_sb[0][0][:, 0:2, :], in_=tf_v[0][:, 0:2, 0:512])
        nc.sync.dma_start(out=tf_sb[0][0][:, 2:4, :], in_=tf_v[0][:, 2:4, 0:512])
        load_q(0)
        nc.sync.dma_start(out=e_sb[:, 1024:4096].bitcast(I32), in_=e_words[0][:, 1024:4096].bitcast(I32))
        nc.sync.dma_start(out=tf_sb[0][1][:], in_=tf_v[0][:, :, 512:1024])
        nc.sync.dma_start(out=z_sb[1][:], in_=z_v[1])
        load_q(1)
        nc.sync.dma_start(out=tf_sb[0][2][:], in_=tf_v[0][:, :, 1024:1536])
        load_q(2)
        nc.sync.dma_start(out=tf_sb[0][3][:], in_=tf_v[0][:, :, 1536:2048])
        load_q(3)
        for c in range(NC):
            nc.sync.dma_start(out=tf_sb[1][c][:], in_=tf_v[1][:, :, 512 * c : 512 * c + 512])

        nc.scalar.activation(out=dummy[:], in_=dummy[:], func=ACT.Abs_reciprocal_sqrt)

        def word_transposes(words, offsets, pool=ps_e, name="ext"):
            bank = pool.tile([P, 4, P], F32, name=name)
            for i in range(2):
                for u in range(2):
                    nc.tensor.transpose(bank[:, 2 * i + u, :], words[:, offsets[i] + u : offsets[i] + 256 : 2], ident[:])
            return bank

        def word_copy(eng, bank, grouped, half):
            dst = grouped[:, 256 * half : 256 * half + 256, :].rearrange("p (i r) t -> p i (r t)", i=2).bitcast(F32)
            dst = dst.rearrange("p i (r u) -> p i r u", u=2)
            srcv = bank[:].rearrange("p (i u) r -> p i r u", u=2)
            if eng == "v":
                nc.vector.tensor_copy(out=dst, in_=srcv)
            else:
                nc.scalar.copy(out=dst, in_=srcv)

        def quant(codes, scales, grouped, lo, hi):
            nc.vector.quantize_mx(
                out=codes[:, lo:hi].bitcast(FP8X4),
                scales=scales[:, lo:hi],
                in_=grouped[:, lo:hi, :].rearrange("p w t -> p (w t)"),
            )

        def z_words(g):
            return z_sb[g][:].rearrange("p s k -> p (s k)").bitcast(F32)

        qg = [keep.tile([P, 512, 4], BF16, name="qg%d" % c, align_bytes=64) for c in range(NC)]
        qc = [keep.tile([P, 512], U32, name="qc%d" % c, align_bytes=64) for c in range(NC)]
        qs = [keep.tile([P, 512], U8, name="qs%d" % c, align_bytes=64) for c in range(NC)]
        gc = [keep.tile([P, 512], U32, name="gc%d" % u, align_bytes=64) for u in range(NG * NC)]
        gs = [keep.tile([P, 512], U8, name="gs%d" % u, align_bytes=64) for u in range(NG * NC)]

        sim, tt, rr, yy, xx, gg = {}, {}, {}, {}, {}, {}

        def mm1(j):
            g, c, s = j // 16, (j % 16) // 4, j % 4
            sim[j] = ps_s.tile([P, 512], F32, name="sim")
            nc.tensor.matmul_mx(
                out=sim[j][:],
                lhsT=zc[g][:, P * s : P * s + P].bitcast(FP8X4),
                lhsT_scale=zs[g][:, P * s : P * s + P],
                rhs=e_sb[:, 1024 * c : 1024 * c + 1024].bitcast(FP4X4),
                rhs_scale=es_sb[:, 512 * c : 512 * c + 512],
                start=True,
                stop=True,
            )

        def tf_view(j):
            g, c, s = j // 16, (j % 16) // 4, j % 4
            return tf_sb[g][c][:, s, :].rearrange("p (k t) -> p t k", t=4)

        def stt1(j):
            tt[j] = work.tile([P, 4, P], F32, name="tt")
            nc.vector.scalar_tensor_tensor(out=tt[j][:], in0=sim[j][:].rearrange("p (k t) -> p t k", t=4), scalar=0.3,
                                           in1=tf_view(j), op0=ALU.max, op1=ALU.add)

        def sq(j):
            g, s = j // 16, j % 4
            rr[j] = work.tile([P, 4, P], F32, name="rr")
            sl = 4 * g + s
            if j in POOL_SQ:
                nc.scalar.activation(out=rr[j][:], in_=tt[j][:], func=ACT.Abs_reciprocal_sqrt,
                                     scale=sinv[:, sl : sl + 1], bias=binv[:, sl : sl + 1])
            else:
                nc.scalar.activation(out=rr[j][:], in_=tt[j][:], func=ACT.Square, scale=sinv[:, sl : sl + 1],
                                     bias=binv[:, sl : sl + 1])

        def ars(j):
            yy[j] = work.tile([P, 4, P], F32, name="yy")
            if j in POOL_SQ:
                nc.gpsimd.tensor_tensor(out=yy[j][:], in0=rr[j][:], in1=rr[j][:], op=ALU.mult)
            else:
                nc.scalar.activation(out=yy[j][:], in_=rr[j][:], func=ACT.Abs_reciprocal_sqrt)

        def tr(j):
            xx[j] = ps_x.tile([P, 4, P], F32, name="xx")
            for t in range(4):
                nc.tensor.transpose(xx[j][:, t, :], yy[j][:, t, :], ident[:])

        def grouped(j):
            u, s = j // 4, j % 4
            if u not in gg:
                gg[u] = gpool.tile([P, 512, 4], BF16, name="gg", align_bytes=64)
            return gg[u][:, P * s : P * s + P, :]

        def rd(j):
            nc.vector.scalar_tensor_tensor(out=grouped(j), in0=xx[j][:].rearrange("p t d -> p d t"), scalar=A_INV,
                                           in1=idfn[:, (j % 16) // 4, :].unsqueeze(1).to_broadcast([P, P, 4]), op0=ALU.subtract, op1=ALU.mult)

        acc, osb, tb = {}, {}, {}
        pg = [keep.tile([P, 512, 4], BF16, name="pg%d" % g, align_bytes=64) for g in range(NG)]
        pc = [keep.tile([P, 512], U32, name="pc%d" % g, align_bytes=64) for g in range(NG)]
        pss = [keep.tile([P, 512], U8, name="pss%d" % g, align_bytes=64) for g in range(NG)]

        def mm2(g, mt, c):
            if c == 0:
                acc[g, mt] = ps_e.tile([P, 512], F32, name="ext") if mt == 3 else ps_a.tile([P, 512], F32, name="acc")
            nc.tensor.matmul_mx(
                out=acc[g, mt][:],
                lhsT=qc[c][:, P * mt : P * mt + P].bitcast(FP8X4),
                lhsT_scale=qs[c][:, P * mt : P * mt + P],
                rhs=gc[NC * g + c][:].bitcast(FP8X4),
                rhs_scale=gs[NC * g + c][:],
                start=(c == 0),
                stop=(c == NC - 1),
            )

        opair = {}

        def out_copy(eng, g, mt):
            if mt % 2 == 0:
                opair[g, mt // 2] = keep.tile([P, 2, 512], F32, name="osb%d_%d" % (g, mt))
            osb[g, mt] = opair[g, mt // 2][:, mt % 2, :]
            dst = osb[g, mt].rearrange("p (k t) -> p k t", t=4)
            srcv = acc[g, mt][:].rearrange("p (t k) -> p k t", t=4)
            if eng == "v":
                nc.vector.tensor_copy(out=dst, in_=srcv)
            else:
                nc.scalar.copy(out=dst, in_=srcv)
            if mt % 2 == 1:
                h = mt // 2
                nc.sync.dma_start(
                    out=out_0[256 * h : 256 * h + 256, 512 * g : 512 * g + 512].rearrange("(i p) n -> p i n", p=P),
                    in_=opair[g, h][:],
                )

        def out_tr(g, mt, pool, name):
            tb[g, mt] = pool.tile([P, 4, P], F32, name=name)
            for t in range(4):
                nc.tensor.transpose(tb[g, mt][:, t, :], osb[g, mt][:, t:512:4], ident[:])

        def p_copy(eng, g, mt):
            dst = pg[g][:, P * mt : P * mt + P, :]
            srcv = tb[g, mt][:].rearrange("p t m -> p m t")
            if eng == "v":
                nc.vector.tensor_copy(out=dst, in_=srcv)
            else:
                nc.scalar.copy(out=dst, in_=srcv)

        def p_quant(g, lo, hi):
            quant(pc[g], pss[g], pg[g], lo, hi)
            nc.sync.dma_start(
                out=out_1[g].rearrange("p m t -> p (m t)")[:, 4 * lo : 4 * hi].bitcast(I32),
                in_=pc[g][:, lo:hi].bitcast(I32),
            )

        def p_scales(g):
            for qd in range(4):
                eng = nc.sync if (qd % 2 == 0 or g == 0) else nc.scalar
                eng.dma_start(
                    out=out_2[g][4 * qd : 4 * qd + 4, :].bitcast(I32),
                    in_=pss[g][32 * qd : 32 * qd + 4, :].bitcast(I32),
                )

        pe_x, act_x, vec_x = {}, {}, {}

        def at(d, j, f):
            d.setdefault(j, []).append(f)

        banks = {}

        def q_words(c):
            return q_sb[c][:].rearrange("p t v -> p (t v)").bitcast(F32)

        def q_tr(c, h):
            banks["q", c, h] = word_transposes(q_words(c), [512 * h, 512 * h + 256])

        def z_tr(h):
            banks["z", h] = word_transposes(z_words(1), [512 * h, 512 * h + 256])

        obf = [keep.tile([P, 2, 512], BF16, name="obf%d" % h) for h in range(2)]

        def o_round(mt):
            nc.gpsimd.tensor_scalar(out=obf[mt // 2][:, mt % 2, :], in0=osb[0, mt], scalar1=1.0, scalar2=0.0, op0=ALU.mult, op1=ALU.add)

        def o_tr(h, pool, name):
            banks["o", h] = word_transposes(obf[h][:].rearrange("p i n -> p (i n)").bitcast(F32), [0, 256], pool, name)

        tr_x, mm_x = {}, {}
        for k, (kind, h) in enumerate((kind, h) for kind in ("q0", "z", "q1", "q2", "q3") for h in range(2)):
            if kind == "z":
                at(tr_x, k, lambda h=h: z_tr(h))
                at(act_x, k, lambda h=h: word_copy("a", banks["z", h], zg[1], h))
                if h == 1:
                    at(vec_x, k + 1, lambda: quant(zc[1], zs[1], zg[1], 0, 512))
            else:
                c = int(kind[1])
                at(tr_x, k, lambda c=c, h=h: q_tr(c, h))
                at(act_x, k, lambda c=c, h=h: word_copy("a", banks["q", c, h], qg[c], h))
                if h == 1:
                    at(vec_x, k + (Q0D if c == 0 else 1), lambda c=c: quant(qc[c], qs[c], qg[c], 0, 512))
        for u in range(NG * NC - 1):
            at(vec_x, 2 * u + 3, lambda u=u: quant(gc[u], gs[u], gg[u], 0, 512))
        for k, g, mt, c in (
            (3, 0, 0, 0), (3, 0, 1, 0), (4, 0, 2, 0), (6, 0, 0, 1), (7, 0, 1, 1), (7, 0, 2, 1), (8, 0, 0, 2), (8, 0, 1, 2), (9, 0, 2, 2),
            (10, 0, 0, 3), (10, 0, 1, 3), (10, 0, 2, 3), (11, 0, 3, 0), (11, 0, 3, 1), (11, 0, 3, 2), (11, 0, 3, 3),
            (12, 1, 0, 0), (12, 1, 1, 0), (13, 1, 0, 1), (13, 1, 1, 1), (13, 1, 2, 0), (14, 1, 2, 1),
            (15, 1, 0, 2), (15, 1, 1, 2), (15, 1, 2, 2), (16, 1, 3, 0), (16, 1, 3, 1), (16, 1, 3, 2),
        ):
            at(mm_x, k, lambda g=g, mt=mt, c=c: mm2(g, mt, c))
        for mt in range(4):
            at(act_x, OC0 + mt, lambda mt=mt: out_copy("a", 0, mt))
            at(act_x, OC0 + mt, lambda mt=mt: o_round(mt))
        for h in range(2):
            at(tr_x, 14 + h, lambda h=h: o_tr(h, ps_e, "ext"))
            at(act_x, 14 + h, lambda h=h: word_copy("a", banks["o", h], pg[0], h))

        PAIRS = BLOCKS // 2
        def const_ops():
            return [
                lambda: nc.vector.tensor_scalar(out=nlen[:], in0=r_sb[:].rearrange("p g t -> p (g t)"), scalar1=0.75, scalar2=0.25, op0=ALU.mult, op1=ALU.add),
                lambda: nc.vector.tensor_scalar(out=nlen2[:], in0=nlen[:], scalar1=1.2, scalar2=None, op0=ALU.mult),
                lambda: nc.vector.reciprocal(out=invn[:], in_=nlen2[:]),
                lambda: nc.vector.tensor_scalar(out=sinv[:], in0=invn[:], scalar1=A_SCALE, scalar2=None, op0=ALU.mult),
                lambda: nc.vector.tensor_scalar(out=binv[:], in0=sinv[:], scalar1=-0.3, scalar2=A_SCALE, op0=ALU.mult, op1=ALU.add),
            ]

        def z0(s, eng):
            zbank = ps_e.tile([P, 2, P], F32, name="ext") if s == 3 else ps_a.tile([P, 2, P], F32, name="acc")
            for u in range(2):
                nc.tensor.transpose(zbank[:, u, :], z_words(0)[:, 256 * s + u : 256 * s + 256 : 2], ident[:])
            dst = zg[0][:, P * s : P * s + P, :].rearrange("p r t -> p (r t)").bitcast(F32).rearrange("p (r u) -> p r u", u=2)
            if eng == "v":
                nc.vector.tensor_copy(out=dst, in_=zbank[:].rearrange("p u r -> p r u"))
            else:
                nc.scalar.copy(out=dst, in_=zbank[:].rearrange("p u r -> p r u"))

        cop = const_ops()
        cop[0]()
        z0(0, "v")
        cop[1]()
        z0(1, "a")
        quant(zc[0], zs[0], zg[0], 0, P)
        cop[2]()
        z0(2, "v")
        z0(3, "a")
        mm1(0)
        quant(zc[0], zs[0], zg[0], P, 2 * P)
        mm1(1)
        cop[3]()
        quant(zc[0], zs[0], zg[0], 2 * P, 3 * P)
        cop[4]()
        quant(zc[0], zs[0], zg[0], 3 * P, 4 * P)
        for k in range(PAIRS + 1):
            solo = k in (0, PAIRS - 1)
            if k < PAIRS:
                stt1(2 * k)
                stt1(2 * k + 1)
                sq(2 * k)
                if solo:
                    ars(2 * k)
                sq(2 * k + 1)
                if solo:
                    ars(2 * k + 1)
            if k == 0:
                nc.vector.tensor_scalar(out=idfn[:].rearrange("p c t -> p (c t)"), in0=idf_sb[:].rearrange("p c t -> p (c t)"), scalar1=-2.2 * A_SCALE, scalar2=None, op0=ALU.mult)
            if k < MM_FIRST:
                mm1(2 * k + 2)
                mm1(2 * k + 3)
            if k > 0:
                tr(2 * k - 2)
                tr(2 * k - 1)
            if k not in EXT_LAST:
                for f in tr_x.get(k, []):
                    f()
            if MM_FIRST <= k < PAIRS - 1:
                mm1(2 * k + 2)
                mm1(2 * k + 3)
            if k in EXT_LAST:
                for f in tr_x.get(k, []):
                    f()
            for f in vec_x.get(k, []):
                f()
            for f in mm_x.get(k, []):
                f()
            if k == PAIRS:
                quant(gc[7], gs[7], gg[7], 0, 256)
                p_quant(0, 0, 512)
                p_scales(0)
            if k > 0:
                rd(2 * k - 2)
                rd(2 * k - 1)
            if k < PAIRS and not solo:
                ars(2 * k)
                ars(2 * k + 1)
            for f in act_x.get(k, []):
                f()
        quant(gc[7], gs[7], gg[7], 256, 512)

        for mt in range(4):
            mm2(1, mt, 3)
        for mt in range(4):
            out_copy("va"[mt % 2], 1, mt)
        for mt in range(4):
            if mt % 2 == 0:
                out_tr(1, mt, ps_s, "sim")
            else:
                out_tr(1, mt, ps_x, "xx")
            p_copy("va"[mt % 2], 1, mt)
            if mt % 2 == 1:
                p_quant(1, 128 * (mt - 1), 128 * (mt + 1))
        p_scales(1)
